import numpy as np
import ml_dtypes


def mxq(x, axis, fmt="e4m3"):
    dtype, down = {"e4m3": (ml_dtypes.float8_e4m3fn, 7), "e5m2": (ml_dtypes.float8_e5m2, 14)}[fmt]
    v = np.moveaxis(np.asarray(x, np.float32).astype(ml_dtypes.bfloat16).astype(np.float64), axis, -1)
    blocks = v.reshape(v.shape[:-1] + (-1, 32))
    amax = np.abs(blocks).max(-1, keepdims=True)
    byte = np.maximum(np.where(amax > 0, np.frexp(amax)[1] - 1 + 127, 0) - down, 1)
    scale = np.exp2(byte - 127.0)
    codes = (blocks / scale).astype(np.float32).astype(dtype).astype(np.float64)
    return np.moveaxis((codes * scale).reshape(v.shape), -1, axis)


WIDE = False


def mx_kscale(k):
    if not WIDE:
        return np.ones(k)
    levels = np.array([30, -30])
    if k % 512:
        return np.exp2(np.random.permutation(np.resize(levels, k // 32))).repeat(32)
    a = np.empty((k // 512, 16))
    for p in range(k // 512):
        a[p, :8] = np.random.permutation(np.resize(levels, 8))
        for g in range(8):
            far = levels[np.abs(levels - a[p, g]) >= 10]
            a[p, g + 8] = far[np.random.randint(len(far))]
    return np.exp2(a.ravel()).repeat(32)


def f64(x):
    return np.asarray(x).astype(np.float64)


def striped(idx):
    return np.tile(np.asarray(idx).reshape(-1, 16).T, (8, 1)).astype(np.uint16)


def unstriped(offs):
    return offs[:16].T.reshape(-1).astype(np.int64)


E2M1 = np.array([0.0, 0.5, 1.0, 1.5, 2.0, 3.0, 4.0, 6.0, -0.0, -0.5, -1.0, -1.5, -2.0, -3.0, -4.0, -6.0])


def pack_weight(w, fmt):
    k, n = w.shape
    w = f64(np.asarray(w, np.float32).astype(ml_dtypes.bfloat16)).reshape(k // 32, 32, n)
    amax = np.abs(w).max(1)
    if fmt in ("e4m3", "e5m2"):
        byte = np.frexp(amax)[1] - 1 + 127 - (7 if fmt == "e4m3" else 14)
    else:
        mant, ex = np.frexp(amax / 6.0)
        byte = np.where(mant > 0.5, ex, ex - 1) + 127
    byte = np.clip(np.where(amax > 0, byte, 1), 1, 254)
    scaled = (w * np.exp2(127.0 - byte)[:, None, :]).reshape(k, n).astype(np.float32)
    by_word = np.ascontiguousarray(scaled.reshape(k // 512, 128, 4, n).transpose(0, 1, 3, 2))
    if fmt in ("e4m3", "e5m2"):
        words = by_word.astype(ml_dtypes.float8_e4m3fn if fmt == "e4m3" else ml_dtypes.float8_e5m2).view(np.uint8)
    else:
        c = by_word.astype(ml_dtypes.float4_e2m1fn).view(np.uint8) & 0xF
        words = (c[..., 0::2] | (c[..., 1::2] << 4)).reshape(k // 512, 128, 2 * n)
    return np.ascontiguousarray(words), np.ascontiguousarray(byte.astype(np.uint8).reshape(k // 512, 16, n))


def unpack_weight(words, scales, fmt):
    g, _, n = scales.shape
    words = np.ascontiguousarray(words).reshape(g, 128, n, -1)
    if fmt in ("e4m3", "e5m2"):
        vals = words.view(ml_dtypes.float8_e4m3fn if fmt == "e4m3" else ml_dtypes.float8_e5m2).astype(np.float64)
    else:
        nib = np.empty((g, 128, n, 4), np.uint8)
        nib[..., 0::2] = words & 0xF
        nib[..., 1::2] = words >> 4
        vals = E2M1[nib]
    vals = vals * np.repeat(np.exp2(scales.astype(np.float64) - 127.0), 8, axis=1)[..., None]
    return vals.transpose(0, 1, 3, 2).reshape(g * 512, n)


K, T, J, R, O, N, E = 512, 2048, 256, 512, 128, 256, 1024


def setup_inputs():
    n = np.random.standard_normal
    idx = np.random.permutation(T)[:J]
    idx2 = np.random.permutation(T)[:J]
    idx3 = np.random.permutation(J)[:O]
    idx4 = np.random.permutation(J)[:O]
    idx5 = np.random.permutation(E)[:O]
    fk = mx_kscale(K)
    fr = mx_kscale(R)
    xtp = pack_weight(n((K, T)) / fk[:, None], "e2m1")
    wp = pack_weight(n((K, R)) * 1 / np.sqrt(K) * fk[:, None] * fr, "e4m3")
    w2p = pack_weight(n((K, R)) * 1 / np.sqrt(K) * fk[:, None] * fr, "e5m2")
    wbp = pack_weight(n((R, N)) * 1 / np.sqrt(R) / fr[:, None], "e2m1")
    return {
        "xt_words": xtp[0],
        "xt_scales": xtp[1],
        "w_words": wp[0],
        "w_scales": wp[1],
        "w2_words": w2p[0],
        "w2_scales": w2p[1],
        "wb_words": wbp[0],
        "wb_scales": wbp[1],
        "offs": striped(idx),
        "offs2": striped(idx2),
        "offs3": striped(idx3),
        "offs4": striped(idx4),
        "offs5": striped(idx5),
    }


def reference(xt_words, xt_scales, w_words, w_scales, w2_words, w2_scales, wb_words, wb_scales, offs, offs2, offs3, offs4, offs5):
    idx = unstriped(offs)
    idx2 = unstriped(offs2)
    idx3 = unstriped(offs3)
    idx4 = unstriped(offs4)
    idx5 = unstriped(offs5)
    xtu = unpack_weight(xt_words, xt_scales, "e2m1")
    wu = unpack_weight(w_words, w_scales, "e4m3")
    w2u = unpack_weight(w2_words, w2_scales, "e5m2")
    wbu = unpack_weight(wb_words, wb_scales, "e2m1")
    xtidxg = xtu[:, idx]
    a = wu.T @ xtidxg
    xtidx2g = xtu[:, idx2]
    b = w2u.T @ xtidx2g
    hid = np.maximum(a[:, idx3], b[:, idx4])
    hidq = mxq(hid, 0, "e5m2")
    p = wbu.T @ hidq
    y = np.zeros((N, E))
    y[:, idx5] = p
    return y

@@ -1,0 +1,158 @@
+from contextlib import ExitStack
+
+import concourse.mybir as mybir
+
+K, T, J, R, O, N, E = 512, 2048, 256, 512, 128, 256, 1024
+FLOPS = 2 * (2 * K * R * J) + 2 * R * N * O
+
+F32 = mybir.dt.float32
+BF16 = mybir.dt.bfloat16
+I32 = mybir.dt.int32
+U32 = mybir.dt.uint32
+U16 = mybir.dt.uint16
+U8 = mybir.dt.uint8
+E4M3 = mybir.dt.float8_e4m3fn_x4
+E5M2 = mybir.dt.float8_e5m2_x4
+E2M1 = mybir.dt.float4_e2m1fn_x4
+COPY = mybir.ActivationFunctionType.Copy
+MAX = mybir.AluOpType.max
+
+P = 128
+PACK = 4
+
+
+def tile_list_ahead_looked_one_scattered_kernel(
+    tc, xt_words, xt_scales, w_words, w_scales, w2_words, w2_scales, wb_words, wb_scales,
+    offs, offs2, offs3, offs4, offs5, out,
+):
+    nc = tc.nc
+    with ExitStack() as ctx:
+        sb = ctx.enter_context(tc.tile_pool(name="sb", bufs=1))
+        ps = ctx.enter_context(tc.psum_pool(name="ps", bufs=1))
+
+        def tile(shape, dtype, name):
+            return sb.tile(shape, dtype, name=name, align_bytes=64)
+
+        def load_scale_rows(queue, plane, scales, q):
+            queue.dma_start(out=plane[32 * q : 32 * q + 4, :].bitcast(I32), in_=scales[0, 4 * q : 4 * q + 4, :].bitcast(I32))
+
+        def load_list(src, name):
+            dst = sb.tile(list(src.shape), U16, name=name)
+            nc.sync.dma_start(dst[:], src)
+            return dst
+
+        xs = tile([P, T], U8, "xs")
+        wsc = tile([P, 2 * R + N], U8, "wsc")
+        ws_raw, w2s_raw, wbs = wsc[:, 0:R], wsc[:, R : 2 * R], wsc[:, 2 * R : 2 * R + N]
+        nc.gpsimd.memset(xs[:].bitcast(I32), 0)
+        nc.vector.memset(wsc[:].bitcast(I32), 0)
+
+        xw = tile([P, T], U16, "xw")
+        ww = tile([P, R], U32, "ww")
+        w2w = tile([P, R], U32, "w2w")
+        wbw = tile([P, 2 * N], U8, "wbw")
+
+        list1 = load_list(offs, "list1")
+        nc.sync.dma_start(out=xw[:].bitcast(I32), in_=xt_words[0].bitcast(I32))
+        list2 = load_list(offs2, "list2")
+        nc.sync.dma_start(out=ww[:].bitcast(I32), in_=w_words[0].rearrange("p n t -> p (n t)").bitcast(I32))
+        for q in range(4):
+            load_scale_rows(nc.sync, xs[:], xt_scales, q)
+        for q in range(4):
+            load_scale_rows(nc.sync, ws_raw, w_scales, q)
+        nc.sync.dma_start(out=w2w[:].bitcast(I32), in_=w2_words[0].rearrange("p n t -> p (n t)").bitcast(I32))
+        for q in range(4):
+            load_scale_rows(nc.sync, w2s_raw, w2_scales, q)
+        list3 = load_list(offs3, "list3")
+        list4 = load_list(offs4, "list4")
+        list5 = load_list(offs5, "list5")
+        for q in range(4):
+            load_scale_rows(nc.gpsimd, wbs, wb_scales, q)
+        nc.gpsimd.dma_start(out=wbw[:].bitcast(I32), in_=wb_words[0].bitcast(I32))
+
+        pages = [tile([P, E], F32, "page%d" % h) for h in range(2)]
+        for page in pages:
+            nc.vector.memset(page[:], 0.0)
+
+        def deal_words(raw, name):
+            dealt = tile([P, PACK, P], U32, name)
+            nc.scalar.copy(
+                out=dealt[:].rearrange("p t (c i) -> p c t i", i=4),
+                in_=raw[:].rearrange("p (c i t) -> p c t i", i=4, t=PACK),
+            )
+            return dealt
+
+        def deal_scales(raw, name):
+            dealt = tile([P, PACK, P], U8, name)
+            nc.vector.tensor_copy(
+                out=dealt[:].rearrange("p t (c i) -> p c t i", i=16),
+                in_=raw.rearrange("p (c i t) -> p c t i", i=16, t=PACK),
+            )
+            return dealt
+
+        def gather(table, lst, dtype, name):
+            picked = tile([P, J], dtype, name)
+            nc.vector.tensor_copy(picked[:], table[:].indirect(lst[:]))
+            return picked
+
+        def first_product(words, scales, fmt, xw_g, xs_g, name):
+            banks = []
+            for t in range(PACK):
+                bank = ps.tile([P, J], F32, name="%s%d" % (name, t), tag="%s%d" % (name, t))
+                nc.tensor.matmul_mx(
+                    out=bank[:], lhsT=words[:, t, :].bitcast(fmt), lhsT_scale=scales[:, t, :],
+                    rhs=xw_g[:].bitcast(E2M1), rhs_scale=xs_g[:], start=True, stop=True,
+                )
+                banks.append(bank)
+            return banks
+
+        xs1 = gather(xs, list1, U8, "xs1")
+        xw1 = gather(xw, list1, U16, "xw1")
+        ws = deal_scales(ws_raw, "ws")
+        wd = deal_words(ww, "wd")
+        a_banks = first_product(wd, ws, E4M3, xw1, xs1, "a")
+        xs2 = gather(xs, list2, U8, "xs2")
+        xw2 = gather(xw, list2, U16, "xw2")
+        w2s = deal_scales(w2s_raw, "w2s")
+        w2d = deal_words(w2w, "w2d")
+        b_banks = first_product(w2d, w2s, E5M2, xw2, xs2, "b")
+
+        a_sb = [tile([P, J], F32, "a_sb%d" % t) for t in range(PACK)]
+        b_sb = [tile([P, J], F32, "b_sb%d" % t) for t in range(PACK)]
+        a_pick = tile([P, PACK, O], F32, "a_pick")
+        b_pick = tile([P, PACK, O], F32, "b_pick")
+        for t in range(PACK + 1):
+            if t < PACK:
+                nc.scalar.activation(a_sb[t][:], a_banks[t][:], COPY)
+            if t > 0:
+                nc.scalar.activation(a_pick[:, t - 1, :], a_sb[t - 1][:].indirect(list3[:]), COPY)
+        last = PACK - 1
+        for t in range(PACK):
+            if t < last:
+                nc.vector.tensor_copy(b_sb[t][:], b_banks[t][:])
+            if t > 0:
+                nc.vector.tensor_copy(b_pick[:, t - 1, :], b_sb[t - 1][:].indirect(list4[:]))
+        nc.scalar.activation(b_sb[last][:], b_banks[last][:], COPY)
+        nc.scalar.activation(b_pick[:, last, :], b_sb[last][:].indirect(list4[:]), COPY)
+
+        hid = tile([P, O, PACK], BF16, "hid")
+        nc.vector.tensor_tensor(hid[:], a_pick[:].rearrange("p t o -> p o t"), b_pick[:].rearrange("p t o -> p o t"), MAX)
+        hid_words = tile([P, O], U32, "hid_words")
+        hid_scales = tile([P, O], U8, "hid_scales")
+        nc.vector.quantize_mx(out=hid_words[:].bitcast(E5M2), scales=hid_scales[:], in_=hid[:].rearrange("p o t -> p (o t)"))
+
+        for h in range(2):
+            bank = ps.tile([P, O], F32, name="p%d" % h, tag="a%d" % h)
+            nc.tensor.matmul_mx(
+                out=bank[:], lhsT=wbw[:, 2 * P * h : 2 * P * (h + 1)].bitcast(E2M1), lhsT_scale=wbs[:, P * h : P * (h + 1)],
+                rhs=hid_words[:].bitcast(E5M2), rhs_scale=hid_scales[:], start=True, stop=True,
+            )
+            p_sb = tile([P, O], F32, "p_sb%d" % h)
+            if h == 0:
+                nc.vector.tensor_copy(p_sb[:], bank[:])
+                nc.vector.tensor_copy(pages[h][:].indirect(list5[:]), p_sb[:])
+                nc.sync.dma_start(out=out[P * h : P * (h + 1), :], in_=pages[h][:])
+            else:
+                nc.scalar.activation(p_sb[:], bank[:], COPY)
+                nc.scalar.activation(pages[h][:].indirect(list5[:]), p_sb[:], COPY)
+                nc.scalar.dma_start(out=out[P * h : P * (h + 1), :], in_=pages[h][:])

@@ -44,7 +44,7 @@ def tile_list_ahead_looked_one_scattered_kernel(
         xs = tile([P, T], U8, "xs")
         wsc = tile([P, 2 * R + N], U8, "wsc")
         ws_raw, w2s_raw, wbs = wsc[:, 0:R], wsc[:, R : 2 * R], wsc[:, 2 * R : 2 * R + N]
-        nc.gpsimd.memset(xs[:].bitcast(I32), 0)
+        nc.vector.memset(xs[:].bitcast(I32), 0)
         nc.vector.memset(wsc[:].bitcast(I32), 0)
 
         xw = tile([P, T], U16, "xw")
@@ -52,27 +52,27 @@ def tile_list_ahead_looked_one_scattered_kernel(
         w2w = tile([P, R], U32, "w2w")
         wbw = tile([P, 2 * N], U8, "wbw")
 
+        nc.gpsimd.dma_start(out=ww[:].bitcast(I32), in_=w_words[0].rearrange("p n t -> p (n t)").bitcast(I32))
+        nc.gpsimd.dma_start(out=w2w[:].bitcast(I32), in_=w2_words[0].rearrange("p n t -> p (n t)").bitcast(I32))
         list1 = load_list(offs, "list1")
         nc.sync.dma_start(out=xw[:].bitcast(I32), in_=xt_words[0].bitcast(I32))
         list2 = load_list(offs2, "list2")
-        nc.sync.dma_start(out=ww[:].bitcast(I32), in_=w_words[0].rearrange("p n t -> p (n t)").bitcast(I32))
+        list3 = load_list(offs3, "list3")
         for q in range(4):
             load_scale_rows(nc.sync, xs[:], xt_scales, q)
         for q in range(4):
             load_scale_rows(nc.sync, ws_raw, w_scales, q)
-        nc.sync.dma_start(out=w2w[:].bitcast(I32), in_=w2_words[0].rearrange("p n t -> p (n t)").bitcast(I32))
         for q in range(4):
             load_scale_rows(nc.sync, w2s_raw, w2_scales, q)
-        list3 = load_list(offs3, "list3")
         list4 = load_list(offs4, "list4")
-        list5 = load_list(offs5, "list5")
         for q in range(4):
-            load_scale_rows(nc.gpsimd, wbs, wb_scales, q)
-        nc.gpsimd.dma_start(out=wbw[:].bitcast(I32), in_=wb_words[0].bitcast(I32))
+            load_scale_rows(nc.sync, wbs, wb_scales, q)
+        nc.sync.dma_start(out=wbw[:].bitcast(I32), in_=wb_words[0].bitcast(I32))
+        list5 = load_list(offs5, "list5")
 
         pages = [tile([P, E], F32, "page%d" % h) for h in range(2)]
         for page in pages:
-            nc.vector.memset(page[:], 0.0)
+            nc.gpsimd.memset(page[:], 0.0)
 
         def deal_words(raw, name):
             dealt = tile([P, PACK, P], U32, name)
@@ -106,34 +106,36 @@ def tile_list_ahead_looked_one_scattered_kernel(
                 banks.append(bank)
             return banks
 
-        xs1 = gather(xs, list1, U8, "xs1")
         xw1 = gather(xw, list1, U16, "xw1")
+        xs1 = gather(xs, list1, U8, "xs1")
         ws = deal_scales(ws_raw, "ws")
         wd = deal_words(ww, "wd")
-        a_banks = first_product(wd, ws, E4M3, xw1, xs1, "a")
-        xs2 = gather(xs, list2, U8, "xs2")
-        xw2 = gather(xw, list2, U16, "xw2")
-        w2s = deal_scales(w2s_raw, "w2s")
         w2d = deal_words(w2w, "w2d")
+        a_banks = first_product(wd, ws, E4M3, xw1, xs1, "a")
+        xw2 = gather(xw, list2, U16, "xw2")
+        xs2 = gather(xs, list2, U8, "xs2")
+        w2s = deal_scales(w2s_raw, "w2s")
         b_banks = first_product(w2d, w2s, E5M2, xw2, xs2, "b")
 
         a_sb = [tile([P, J], F32, "a_sb%d" % t) for t in range(PACK)]
         b_sb = [tile([P, J], F32, "b_sb%d" % t) for t in range(PACK)]
         a_pick = tile([P, PACK, O], F32, "a_pick")
         b_pick = tile([P, PACK, O], F32, "b_pick")
-        for t in range(PACK + 1):
-            if t < PACK:
-                nc.scalar.activation(a_sb[t][:], a_banks[t][:], COPY)
-            if t > 0:
-                nc.scalar.activation(a_pick[:, t - 1, :], a_sb[t - 1][:].indirect(list3[:]), COPY)
-        last = PACK - 1
-        for t in range(PACK):
-            if t < last:
-                nc.vector.tensor_copy(b_sb[t][:], b_banks[t][:])
-            if t > 0:
-                nc.vector.tensor_copy(b_pick[:, t - 1, :], b_sb[t - 1][:].indirect(list4[:]))
-        nc.scalar.activation(b_sb[last][:], b_banks[last][:], COPY)
-        nc.scalar.activation(b_pick[:, last, :], b_sb[last][:].indirect(list4[:]), COPY)
+        def on_vector(out_ap, in_ap):
+            nc.vector.tensor_copy(out_ap, in_ap)
+
+        def on_scalar(out_ap, in_ap):
+            nc.scalar.activation(out_ap, in_ap, COPY)
+
+        jobs = [(a_banks[t], a_sb[t], list3, a_pick[:, t, :]) for t in range(PACK)]
+        jobs.extend([(b_banks[t], b_sb[t], list4, b_pick[:, t, :]) for t in range(PACK)])
+        for move, mine in ((on_vector, jobs[0::2]), (on_scalar, jobs[1::2])):
+            for i in range(len(mine) + 1):
+                if i < len(mine):
+                    move(mine[i][1][:], mine[i][0][:])
+                if i > 0:
+                    bank, whole, lst, picked = mine[i - 1]
+                    move(picked, whole[:].indirect(lst[:]))
 
         hid = tile([P, O, PACK], BF16, "hid")
         nc.vector.tensor_tensor(hid[:], a_pick[:].rearrange("p t o -> p o t"), b_pick[:].rearrange("p t o -> p o t"), MAX)

@@ -30,8 +30,8 @@ def tile_list_ahead_looked_one_scattered_kernel(
         sb = ctx.enter_context(tc.tile_pool(name="sb", bufs=1))
         ps = ctx.enter_context(tc.psum_pool(name="ps", bufs=1))
 
-        def tile(shape, dtype, name):
-            return sb.tile(shape, dtype, name=name, align_bytes=64)
+        def tile(shape, dtype, name, tag=None):
+            return sb.tile(shape, dtype, name=name, tag=tag or name, align_bytes=64)
 
         def load_scale_rows(queue, plane, scales, q):
             queue.dma_start(out=plane[32 * q : 32 * q + 4, :].bitcast(I32), in_=scales[0, 4 * q : 4 * q + 4, :].bitcast(I32))
@@ -42,10 +42,12 @@ def tile_list_ahead_looked_one_scattered_kernel(
             return dst
 
         xs = tile([P, T], U8, "xs")
-        wsc = tile([P, 2 * R + N], U8, "wsc")
-        ws_raw, w2s_raw, wbs = wsc[:, 0:R], wsc[:, R : 2 * R], wsc[:, 2 * R : 2 * R + N]
+        wsc = tile([P, R + N], U8, "wsc")
+        w2s_tile = tile([P, R], U8, "w2s_tile")
+        ws_raw, w2s_raw, wbs = wsc[:, 0:R], w2s_tile[:], wsc[:, R : R + N]
         nc.vector.memset(xs[:].bitcast(I32), 0)
         nc.vector.memset(wsc[:].bitcast(I32), 0)
+        nc.vector.memset(w2s_raw.bitcast(I32), 0)
 
         xw = tile([P, T], U16, "xw")
         ww = tile([P, R], U32, "ww")
@@ -53,7 +55,6 @@ def tile_list_ahead_looked_one_scattered_kernel(
         wbw = tile([P, 2 * N], U8, "wbw")
 
         nc.gpsimd.dma_start(out=ww[:].bitcast(I32), in_=w_words[0].rearrange("p n t -> p (n t)").bitcast(I32))
-        nc.gpsimd.dma_start(out=w2w[:].bitcast(I32), in_=w2_words[0].rearrange("p n t -> p (n t)").bitcast(I32))
         list1 = load_list(offs, "list1")
         nc.sync.dma_start(out=xw[:].bitcast(I32), in_=xt_words[0].bitcast(I32))
         list2 = load_list(offs2, "list2")
@@ -62,17 +63,18 @@ def tile_list_ahead_looked_one_scattered_kernel(
             load_scale_rows(nc.sync, xs[:], xt_scales, q)
         for q in range(4):
             load_scale_rows(nc.sync, ws_raw, w_scales, q)
+        nc.sync.dma_start(out=w2w[:].bitcast(I32), in_=w2_words[0].rearrange("p n t -> p (n t)").bitcast(I32))
         for q in range(4):
             load_scale_rows(nc.sync, w2s_raw, w2_scales, q)
         list4 = load_list(offs4, "list4")
-        for q in range(4):
-            load_scale_rows(nc.sync, wbs, wb_scales, q)
-        nc.sync.dma_start(out=wbw[:].bitcast(I32), in_=wb_words[0].bitcast(I32))
         list5 = load_list(offs5, "list5")
+        for q in range(4):
+            load_scale_rows(nc.gpsimd, wbs, wb_scales, q)
+        nc.gpsimd.dma_start(out=wbw[:].bitcast(I32), in_=wb_words[0].bitcast(I32))
 
         pages = [tile([P, E], F32, "page%d" % h) for h in range(2)]
         for page in pages:
-            nc.gpsimd.memset(page[:], 0.0)
+            nc.vector.memset(page[:], 0.0)
 
         def deal_words(raw, name):
             dealt = tile([P, PACK, P], U32, name)
@@ -117,8 +119,10 @@ def tile_list_ahead_looked_one_scattered_kernel(
         w2s = deal_scales(w2s_raw, "w2s")
         b_banks = first_product(w2d, w2s, E5M2, xw2, xs2, "b")
 
-        a_sb = [tile([P, J], F32, "a_sb%d" % t) for t in range(PACK)]
-        b_sb = [tile([P, J], F32, "b_sb%d" % t) for t in range(PACK)]
+        a_even = tile([P, 2, J], F32, "a_even", tag="w2w")
+        a_odd = tile([P, 2, J], F32, "a_odd", tag="w2s_tile")
+        a_sb = [(a_even, a_odd)[t % 2][:, t // 2, :] for t in range(PACK)]
+        b_sb = [tile([P, J], F32, "b_sb%d" % t)[:] for t in range(PACK)]
         a_pick = tile([P, PACK, O], F32, "a_pick")
         b_pick = tile([P, PACK, O], F32, "b_pick")
         def on_vector(out_ap, in_ap):
@@ -129,13 +133,13 @@ def tile_list_ahead_looked_one_scattered_kernel(
 
         jobs = [(a_banks[t], a_sb[t], list3, a_pick[:, t, :]) for t in range(PACK)]
         jobs.extend([(b_banks[t], b_sb[t], list4, b_pick[:, t, :]) for t in range(PACK)])
-        for move, mine in ((on_vector, jobs[0::2]), (on_scalar, jobs[1::2])):
+        for move, mine in ((on_scalar, jobs[0::2]), (on_vector, jobs[1::2])):
             for i in range(len(mine) + 1):
                 if i < len(mine):
-                    move(mine[i][1][:], mine[i][0][:])
+                    move(mine[i][1], mine[i][0][:])
                 if i > 0:
                     bank, whole, lst, picked = mine[i - 1]
-                    move(picked, whole[:].indirect(lst[:]))
+                    move(picked, whole.indirect(lst[:]))
 
         hid = tile([P, O, PACK], BF16, "hid")
         nc.vector.tensor_tensor(hid[:], a_pick[:].rearrange("p t o -> p o t"), b_pick[:].rearrange("p t o -> p o t"), MAX)

from contextlib import ExitStack

import concourse.mybir as mybir

K, T, J, R, O, N, E = 512, 2048, 256, 512, 128, 256, 1024
FLOPS = 2 * (2 * K * R * J) + 2 * R * N * O

F32 = mybir.dt.float32
BF16 = mybir.dt.bfloat16
I32 = mybir.dt.int32
U32 = mybir.dt.uint32
U16 = mybir.dt.uint16
U8 = mybir.dt.uint8
E4M3 = mybir.dt.float8_e4m3fn_x4
E5M2 = mybir.dt.float8_e5m2_x4
E2M1 = mybir.dt.float4_e2m1fn_x4
COPY = mybir.ActivationFunctionType.Copy
MAX = mybir.AluOpType.max

P = 128
PACK = 4


def tile_list_ahead_looked_one_scattered_kernel(
    tc, xt_words, xt_scales, w_words, w_scales, w2_words, w2_scales, wb_words, wb_scales,
    offs, offs2, offs3, offs4, offs5, out,
):
    nc = tc.nc
    with ExitStack() as ctx:
        sb = ctx.enter_context(tc.tile_pool(name="sb", bufs=1))
        ps = ctx.enter_context(tc.psum_pool(name="ps", bufs=1))

        def tile(shape, dtype, name, tag=None):
            return sb.tile(shape, dtype, name=name, tag=tag or name, align_bytes=64)

        def load_scale_rows(queue, plane, scales, q):
            queue.dma_start(out=plane[32 * q : 32 * q + 4, :].bitcast(I32), in_=scales[0, 4 * q : 4 * q + 4, :].bitcast(I32))

        def load_list(src, name):
            dst = sb.tile(list(src.shape), U16, name=name)
            nc.sync.dma_start(dst[:], src)
            return dst

        xs = tile([P, T], U8, "xs")
        wsc = tile([P, R + N], U8, "wsc")
        w2s_tile = tile([P, R], U8, "w2s_tile")
        ws_raw, w2s_raw, wbs = wsc[:, 0:R], w2s_tile[:], wsc[:, R : R + N]
        nc.vector.memset(xs[:].bitcast(I32), 0)
        nc.vector.memset(wsc[:].bitcast(I32), 0)
        nc.vector.memset(w2s_raw.bitcast(I32), 0)

        xw = tile([P, T], U16, "xw")
        ww = tile([P, R], U32, "ww")
        w2w = tile([P, R], U32, "w2w")
        wbw = tile([P, 2 * N], U8, "wbw")

        nc.gpsimd.dma_start(out=ww[:].bitcast(I32), in_=w_words[0].rearrange("p n t -> p (n t)").bitcast(I32))
        list1 = load_list(offs, "list1")
        nc.sync.dma_start(out=xw[:].bitcast(I32), in_=xt_words[0].bitcast(I32))
        list2 = load_list(offs2, "list2")
        list3 = load_list(offs3, "list3")
        for q in range(4):
            load_scale_rows(nc.sync, xs[:], xt_scales, q)
        for q in range(4):
            load_scale_rows(nc.sync, ws_raw, w_scales, q)
        nc.sync.dma_start(out=w2w[:].bitcast(I32), in_=w2_words[0].rearrange("p n t -> p (n t)").bitcast(I32))
        for q in range(4):
            load_scale_rows(nc.sync, w2s_raw, w2_scales, q)
        list4 = load_list(offs4, "list4")
        list5 = load_list(offs5, "list5")
        for q in range(4):
            load_scale_rows(nc.gpsimd, wbs, wb_scales, q)
        nc.gpsimd.dma_start(out=wbw[:].bitcast(I32), in_=wb_words[0].bitcast(I32))

        pages = [tile([P, E], F32, "page%d" % h) for h in range(2)]
        for page in pages:
            nc.vector.memset(page[:], 0.0)

        def deal_words(raw, name):
            dealt = tile([P, PACK, P], U32, name)
            nc.scalar.copy(
                out=dealt[:].rearrange("p t (c i) -> p c t i", i=4),
                in_=raw[:].rearrange("p (c i t) -> p c t i", i=4, t=PACK),
            )
            return dealt

        def deal_scales(raw, name):
            dealt = tile([P, PACK, P], U8, name)
            nc.vector.tensor_copy(
                out=dealt[:].rearrange("p t (c i) -> p c t i", i=16),
                in_=raw.rearrange("p (c i t) -> p c t i", i=16, t=PACK),
            )
            return dealt

        def gather(table, lst, dtype, name):
            picked = tile([P, J], dtype, name)
            nc.vector.tensor_copy(picked[:], table[:].indirect(lst[:]))
            return picked

        def first_product(words, scales, fmt, xw_g, xs_g, name):
            banks = []
            for t in range(PACK):
                bank = ps.tile([P, J], F32, name="%s%d" % (name, t), tag="%s%d" % (name, t))
                nc.tensor.matmul_mx(
                    out=bank[:], lhsT=words[:, t, :].bitcast(fmt), lhsT_scale=scales[:, t, :],
                    rhs=xw_g[:].bitcast(E2M1), rhs_scale=xs_g[:], start=True, stop=True,
                )
                banks.append(bank)
            return banks

        xw1 = gather(xw, list1, U16, "xw1")
        xs1 = gather(xs, list1, U8, "xs1")
        ws = deal_scales(ws_raw, "ws")
        wd = deal_words(ww, "wd")
        w2d = deal_words(w2w, "w2d")
        a_banks = first_product(wd, ws, E4M3, xw1, xs1, "a")
        xw2 = gather(xw, list2, U16, "xw2")
        xs2 = gather(xs, list2, U8, "xs2")
        w2s = deal_scales(w2s_raw, "w2s")
        b_banks = first_product(w2d, w2s, E5M2, xw2, xs2, "b")

        a_even = tile([P, 2, J], F32, "a_even", tag="w2w")
        a_odd = tile([P, 2, J], F32, "a_odd", tag="w2s_tile")
        a_sb = [(a_even, a_odd)[t % 2][:, t // 2, :] for t in range(PACK)]
        b_sb = [tile([P, J], F32, "b_sb%d" % t)[:] for t in range(PACK)]
        a_pick = tile([P, PACK, O], F32, "a_pick")
        b_pick = tile([P, PACK, O], F32, "b_pick")
        def on_vector(out_ap, in_ap):
            nc.vector.tensor_copy(out_ap, in_ap)

        def on_scalar(out_ap, in_ap):
            nc.scalar.activation(out_ap, in_ap, COPY)

        jobs = [(a_banks[t], a_sb[t], list3, a_pick[:, t, :]) for t in range(PACK)]
        jobs.extend([(b_banks[t], b_sb[t], list4, b_pick[:, t, :]) for t in range(PACK)])
        for move, mine in ((on_scalar, jobs[0::2]), (on_vector, jobs[1::2])):
            for i in range(len(mine) + 1):
                if i < len(mine):
                    move(mine[i][1], mine[i][0][:])
                if i > 0:
                    bank, whole, lst, picked = mine[i - 1]
                    move(picked, whole.indirect(lst[:]))

        hid = tile([P, O, PACK], BF16, "hid")
        nc.vector.tensor_tensor(hid[:], a_pick[:].rearrange("p t o -> p o t"), b_pick[:].rearrange("p t o -> p o t"), MAX)
        hid_words = tile([P, O], U32, "hid_words")
        hid_scales = tile([P, O], U8, "hid_scales")
        nc.vector.quantize_mx(out=hid_words[:].bitcast(E5M2), scales=hid_scales[:], in_=hid[:].rearrange("p o t -> p (o t)"))

        for h in range(2):
            bank = ps.tile([P, O], F32, name="p%d" % h, tag="a%d" % h)
            nc.tensor.matmul_mx(
                out=bank[:], lhsT=wbw[:, 2 * P * h : 2 * P * (h + 1)].bitcast(E2M1), lhsT_scale=wbs[:, P * h : P * (h + 1)],
                rhs=hid_words[:].bitcast(E5M2), rhs_scale=hid_scales[:], start=True, stop=True,
            )
            p_sb = tile([P, O], F32, "p_sb%d" % h)
            if h == 0:
                nc.vector.tensor_copy(p_sb[:], bank[:])
                nc.vector.tensor_copy(pages[h][:].indirect(list5[:]), p_sb[:])
                nc.sync.dma_start(out=out[P * h : P * (h + 1), :], in_=pages[h][:])
            else:
                nc.scalar.activation(p_sb[:], bank[:], COPY)
                nc.scalar.activation(pages[h][:].indirect(list5[:]), p_sb[:], COPY)
                nc.scalar.dma_start(out=out[P * h : P * (h + 1), :], in_=pages[h][:])
